import numpy as np
import ml_dtypes


def mxq(x, axis, fmt="e4m3"):
    dtype, down = {"e4m3": (ml_dtypes.float8_e4m3fn, 7), "e5m2": (ml_dtypes.float8_e5m2, 14)}[fmt]
    v = np.moveaxis(np.asarray(x, np.float32).astype(ml_dtypes.bfloat16).astype(np.float64), axis, -1)
    blocks = v.reshape(v.shape[:-1] + (-1, 32))
    amax = np.abs(blocks).max(-1, keepdims=True)
    byte = np.maximum(np.where(amax > 0, np.frexp(amax)[1] - 1 + 127, 0) - down, 1)
    scale = np.exp2(byte - 127.0)
    codes = (blocks / scale).astype(np.float32).astype(dtype).astype(np.float64)
    return np.moveaxis((codes * scale).reshape(v.shape), -1, axis)


WIDE = False


def mx_kscale(k):
    if not WIDE:
        return np.ones(k)
    levels = np.array([10, -10, 5, -5, 0])
    if k % 512:
        return np.exp2(np.random.permutation(np.resize(levels, k // 32))).repeat(32)
    a = np.empty((k // 512, 16))
    for p in range(k // 512):
        a[p, :8] = np.random.permutation(np.resize(levels, 8))
        for g in range(8):
            far = levels[np.abs(levels - a[p, g]) >= 10]
            a[p, g + 8] = far[np.random.randint(len(far))]
    return np.exp2(a.ravel()).repeat(32)


def f64(x):
    return np.asarray(x).astype(np.float64)


def striped(idx):
    return np.tile(np.asarray(idx).reshape(-1, 16).T, (8, 1)).astype(np.uint16)


def unstriped(offs):
    return offs[:16].T.reshape(-1).astype(np.int64)


E2M1 = np.array([0.0, 0.5, 1.0, 1.5, 2.0, 3.0, 4.0, 6.0, -0.0, -0.5, -1.0, -1.5, -2.0, -3.0, -4.0, -6.0])


def pack_weight(w, fmt):
    k, n = w.shape
    w = f64(np.asarray(w, np.float32).astype(ml_dtypes.bfloat16)).reshape(k // 32, 32, n)
    amax = np.abs(w).max(1)
    if fmt == "e4m3":
        byte = np.frexp(amax)[1] - 1 + 127 - 7
    else:
        mant, ex = np.frexp(amax / 6.0)
        byte = np.where(mant > 0.5, ex, ex - 1) + 127
    byte = np.clip(np.where(amax > 0, byte, 1), 1, 254)
    scaled = (w * np.exp2(127.0 - byte)[:, None, :]).reshape(k, n).astype(np.float32)
    by_word = np.ascontiguousarray(scaled.reshape(k // 512, 128, 4, n).transpose(0, 1, 3, 2))
    if fmt == "e4m3":
        words = by_word.astype(ml_dtypes.float8_e4m3fn).view(np.uint8)
    else:
        c = by_word.astype(ml_dtypes.float4_e2m1fn).view(np.uint8) & 0xF
        words = (c[..., 0::2] | (c[..., 1::2] << 4)).reshape(k // 512, 128, 2 * n)
    return np.ascontiguousarray(words), np.ascontiguousarray(byte.astype(np.uint8).reshape(k // 512, 16, n))


def unpack_weight(words, scales, fmt):
    g, _, n = scales.shape
    words = np.ascontiguousarray(words).reshape(g, 128, n, -1)
    if fmt == "e4m3":
        vals = words.view(ml_dtypes.float8_e4m3fn).astype(np.float64)
    else:
        nib = np.empty((g, 128, n, 4), np.uint8)
        nib[..., 0::2] = words & 0xF
        nib[..., 1::2] = words >> 4
        vals = E2M1[nib]
    vals = vals * np.repeat(np.exp2(scales.astype(np.float64) - 127.0), 8, axis=1)[..., None]
    return vals.transpose(0, 1, 3, 2).reshape(g * 512, n)


D, E, T, I, Q = 512, 512, 2048, 512, 128


def setup_inputs():
    n = np.random.standard_normal
    idx4 = np.random.permutation(I)[:I]
    idx = np.random.permutation(T)[:I]
    fd = mx_kscale(D)
    fe = mx_kscale(E)
    keysp = pack_weight(n((D, T)) / fd[:, None], "e2m1")
    valsp = pack_weight(n((E, T)) / fe[:, None], "e2m1")
    return {
        "query": (n((D, Q)) * 0.8 / np.sqrt(D) * fd[:, None]).astype(np.float32),
        "keys_words": keysp[0],
        "keys_scales": keysp[1],
        "reserve": (np.random.uniform(0.2, 1.0, (Q, 1))).astype(np.float32),
        "gout": (n((E, Q)) * 1 / np.sqrt(E) * fe[:, None]).astype(np.float32),
        "vals_words": valsp[0],
        "vals_scales": valsp[1],
        "base": (0.5 * n((Q, I))).astype(np.float32),
        "offs4": striped(idx4),
        "offs": striped(idx),
    }


def reference(query, keys_words, keys_scales, reserve, gout, vals_words, vals_scales, base, offs4, offs):
    idx4 = unstriped(offs4)
    idx = unstriped(offs)
    keysu = unpack_weight(keys_words, keys_scales, "e2m1")
    valsu = unpack_weight(vals_words, vals_scales, "e2m1")
    queryq = mxq(f64(query), 0, "e4m3")
    keysidxg = keysu[:, idx]
    a = queryq.T @ keysidxg
    p = np.exp(a - np.max(a, axis=1, keepdims=True))
    r = p / np.sum(p, axis=1, keepdims=True)
    u0 = np.sqrt(r * r[:, idx4])
    goutq = mxq(f64(gout), 0, "e4m3")
    valsidxg = valsu[:, idx]
    c0 = goutq.T @ valsidxg
    du0 = c0 / (np.sum(u0, axis=1, keepdims=True) + f64(reserve)) + np.sum(c0 * u0 / np.square(np.sum(u0, axis=1, keepdims=True) + f64(reserve)) * (-1.0), axis=1, keepdims=True)
    e1 = du0 * 0.5 / np.sqrt(r * r[:, idx4]) * r
    s1 = np.zeros((Q, I))
    s1[:, idx4] = e1
    dr = du0 * 0.5 / np.sqrt(r * r[:, idx4]) * r[:, idx4] + s1
    dp = dr / np.sum(p, axis=1, keepdims=True) + np.sum(dr * p / np.square(np.sum(p, axis=1, keepdims=True)) * (-1.0), axis=1, keepdims=True)
    da = dp * p
    hda = da * 512.0 * 2.0 * 512.0
    hdp = hda * p
    hdr = hdp / np.sum(p, axis=1, keepdims=True) + np.sum(hdp, axis=1, keepdims=True) * (-1.0) / np.square(np.sum(p, axis=1, keepdims=True)) * p
    he1 = hdr[:, idx4]
    hdu0 = hdr * r[:, idx4] / np.sqrt(r * r[:, idx4]) * 0.5 + he1 * r / np.sqrt(r * r[:, idx4]) * 0.5
    hu0 = np.sum(hdu0 * c0 / np.square(np.sum(u0, axis=1, keepdims=True) + f64(reserve)) * (-1.0), axis=1, keepdims=True) + np.sum(hdu0, axis=1, keepdims=True) * (-1.0) / np.square(np.sum(u0, axis=1, keepdims=True) + f64(reserve)) * c0 + np.sum(np.sum(hdu0, axis=1, keepdims=True) * (-1.0) * c0 * u0 / np.square(np.square(np.sum(u0, axis=1, keepdims=True) + f64(reserve))) * (-1.0), axis=1, keepdims=True) * (np.sum(u0, axis=1, keepdims=True) + f64(reserve)) * 2.0
    e51 = hdr * r[:, idx4] * du0 * 0.5 / np.square(np.sqrt(r * r[:, idx4])) * (-1.0) * 0.5 / np.sqrt(r * r[:, idx4]) * r
    s51 = np.zeros((Q, I))
    s51[:, idx4] = e51
    e52 = hdr * du0 * 0.5 / np.sqrt(r * r[:, idx4])
    s52 = np.zeros((Q, I))
    s52[:, idx4] = e52
    e53 = he1 * r * du0 * 0.5 / np.square(np.sqrt(r * r[:, idx4])) * (-1.0) * 0.5 / np.sqrt(r * r[:, idx4]) * r
    s53 = np.zeros((Q, I))
    s53[:, idx4] = e53
    e54 = hu0 * 0.5 / np.sqrt(r * r[:, idx4]) * r
    s54 = np.zeros((Q, I))
    s54[:, idx4] = e54
    hr = hdr * r[:, idx4] * du0 * 0.5 / np.square(np.sqrt(r * r[:, idx4])) * (-1.0) * 0.5 / np.sqrt(r * r[:, idx4]) * r[:, idx4] + he1 * r * du0 * 0.5 / np.square(np.sqrt(r * r[:, idx4])) * (-1.0) * 0.5 / np.sqrt(r * r[:, idx4]) * r[:, idx4] + he1 * du0 * 0.5 / np.sqrt(r * r[:, idx4]) + hu0 * 0.5 / np.sqrt(r * r[:, idx4]) * r[:, idx4] + s51 + s52 + s53 + s54
    hp = hda * dp + np.sum(hdp * dr / np.square(np.sum(p, axis=1, keepdims=True)) * (-1.0), axis=1, keepdims=True) + np.sum(hdp, axis=1, keepdims=True) * (-1.0) / np.square(np.sum(p, axis=1, keepdims=True)) * dr + np.sum(np.sum(hdp, axis=1, keepdims=True) * (-1.0) * dr * p / np.square(np.square(np.sum(p, axis=1, keepdims=True))) * (-1.0), axis=1, keepdims=True) * np.sum(p, axis=1, keepdims=True) * 2.0 + hr / np.sum(p, axis=1, keepdims=True) + np.sum(hr * p / np.square(np.sum(p, axis=1, keepdims=True)) * (-1.0), axis=1, keepdims=True)
    ha = hp * p
    y = ha + f64(base)
    return y

@@ -1,0 +1,265 @@
+from contextlib import ExitStack
+
+import concourse.mybir as mybir
+
+F32 = mybir.dt.float32
+BF16 = mybir.dt.bfloat16
+I32 = mybir.dt.int32
+U32 = mybir.dt.uint32
+U16 = mybir.dt.uint16
+U8 = mybir.dt.uint8
+FP8X4 = mybir.dt.float8_e4m3fn_x4
+FP4X4 = mybir.dt.float4_e2m1fn_x4
+ALU = mybir.AluOpType
+ACT = mybir.ActivationFunctionType
+ADD, SUB, MUL, MAX = ALU.add, ALU.subtract, ALU.mult, ALU.max
+
+P = 128
+PACK = 4
+TOKENS = 2048
+SLOTS = 512
+ROWS = 128
+HALF = SLOTS // 2
+HALVES = (slice(0, HALF), slice(HALF, SLOTS))
+LIST_HALVES = (slice(0, HALF // 16), slice(HALF // 16, SLOTS // 16))
+PENALTY = 512.0 * 2.0 * 512.0
+
+FLOPS = 2 * 2 * 512 * ROWS * SLOTS
+
+
+def tile_attend_gpdirect_agreed_kernel(
+    tc, query, keys_words, keys_scales, reserve, gout, vals_words, vals_scales, base, offs4, offs, out
+):
+    nc = tc.nc
+    vec, act = nc.vector, nc.scalar
+
+    with ExitStack() as ctx:
+        pool = ctx.enter_context(tc.tile_pool(name="sbuf", bufs=1))
+        psum = ctx.enter_context(tc.psum_pool(name="psum", bufs=1))
+
+        def wide(name):
+            return pool.tile([P, SLOTS], F32, name=name)
+
+        def col(name):
+            return pool.tile([P, 1], F32, name=name)
+
+        def cols(name):
+            return [col(name + "_lo"), col(name + "_hi")]
+
+        def stt(dst, in0, scalar, op0, in1, op1, accum=None):
+            vec.scalar_tensor_tensor(dst, in0, scalar, in1, op0, op1, accum_out=accum)
+
+        def tiny(name, in0, s1, op0, s2=None, op1=None):
+            dst = col(name)
+            if op1 is None:
+                vec.tensor_scalar(dst[:], in0[:], s1, None, op0)
+            else:
+                vec.tensor_scalar(dst[:], in0[:], s1, s2, op0, op1)
+            return dst
+
+        token_list = pool.tile([P, SLOTS // 16], U16, name="token_list")
+        slot_list = pool.tile([P, SLOTS // 16], U16, name="slot_list")
+        key_words = pool.tile([P, TOKENS], U16, name="key_words")
+        val_words = pool.tile([P, TOKENS], U16, name="val_words")
+        key_bytes = pool.tile([P, TOKENS], U8, name="key_bytes", tag="key_bytes", align_bytes=64)
+        val_bytes = pool.tile([P, TOKENS], U8, name="val_bytes")
+        res = col("res")
+
+        def load_scale_rows(plane, scales, queues):
+            for quad, queue in enumerate(queues):
+                queue.dma_start(
+                    plane[32 * quad : 32 * quad + 4, :].bitcast(I32),
+                    scales[0, 4 * quad : 4 * quad + 4, :].bitcast(I32),
+                )
+
+        vec.memset(key_bytes[:].bitcast(I32), 0)
+        vec.memset(val_bytes[:].bitcast(I32), 0)
+        def load_rows(name, rows, queue):
+            raw = pool.tile([P, PACK, ROWS], F32, name=name + "_raw", tag=name + "_staging")
+            queue.dma_start(raw[:], rows.rearrange("(p j) w -> p j w", j=PACK))
+            return raw
+
+        act.dma_start(res[:], reserve)
+        nc.sync.dma_start(token_list[:], offs)
+        nc.sync.dma_start(key_words[:].bitcast(I32), keys_words[0].bitcast(I32))
+        load_scale_rows(key_bytes, keys_scales, [nc.sync] * 4)
+        query_raw = load_rows("query", query, nc.sync)
+        gout_raw = load_rows("gout", gout, nc.gpsimd)
+        nc.sync.dma_start(val_words[:].bitcast(I32), vals_words[0].bitcast(I32))
+        load_scale_rows(val_bytes, vals_scales, [nc.sync, nc.sync, nc.gpsimd, nc.gpsimd])
+        nc.sync.dma_start(slot_list[:], offs4)
+        res2 = col("res2")
+        act.activation(res2[:], res[:], ACT.Copy, scale=2.0)
+
+        def quantise(name, raw):
+            grouped = pool.tile([P, ROWS, PACK], BF16, name=name + "_bf16", tag="bf16", align_bytes=64)
+            codes = pool.tile([P, ROWS], U32, name=name + "_codes", align_bytes=64)
+            scales = pool.tile([P, ROWS], U8, name=name + "_scales", align_bytes=64)
+            act.activation(grouped[:], raw[:].rearrange("p j w -> p w j"), ACT.Copy)
+            vec.quantize_mx(
+                out=codes[:].bitcast(FP8X4), scales=scales[:], in_=grouped[:].rearrange("p w j -> p (w j)")
+            )
+            return codes, scales
+
+        def gather_packed(name, words, plane, words_tag):
+            got_words = pool.tile([P, SLOTS], U16, name=name + "_got_words", tag=words_tag, align_bytes=64)
+            got_bytes = pool.tile([P, SLOTS], U8, name=name + "_got_bytes", tag="got_bytes", align_bytes=64)
+            vec.tensor_copy(got_words[:], words[:].indirect(token_list[:]))
+            vec.tensor_copy(got_bytes[:], plane[:].indirect(token_list[:]))
+            return got_words, got_bytes
+
+        def product(name, rows, columns):
+            acc = psum.tile([P, SLOTS], F32, name=name)
+            nc.tensor.matmul_mx(
+                out=acc[:],
+                lhsT=rows[0][:].bitcast(FP8X4),
+                lhsT_scale=rows[1][:],
+                rhs=columns[0][:].bitcast(FP4X4),
+                rhs_scale=columns[1][:],
+                start=True,
+                stop=True,
+            )
+            return acc
+
+        query_mx = quantise("query", query_raw)
+        a = product("a", query_mx, gather_packed("key", key_words, key_bytes, "key_got_words"))
+        gout_mx = quantise("gout", gout_raw)
+        base_sb = pool.tile([P, SLOTS], F32, name="base_sb", tag="gout_staging")
+        nc.sync.dma_start(base_sb[:], base)
+
+        neg_max = col("neg_max")
+        vec.tensor_reduce(neg_max[:], a[:], mybir.AxisListType.X, MAX, negate=True)
+        p = wide("p")
+        p_sum = col("p_sum")
+        act.activation(p[:], a[:], ACT.Exp, bias=neg_max[:], accum_out=p_sum[:])
+
+        root = col("root")
+        act.activation(root[:], p_sum[:], ACT.Abs_reciprocal_sqrt)
+        res_s = col("res_s")
+        act.activation(res_s[:], res2[:], ACT.Copy, scale=root[:])
+
+        c0 = product("c0", gout_mx, gather_packed("val", val_words, val_bytes, "key_bytes"))
+
+        inv_p = col("inv_p")
+        vec.reciprocal(inv_p[:], p_sum[:])
+        r = wide("r")
+        vec.tensor_scalar(r[:], p[:], inv_p[:], None, MUL)
+        y_scale = tiny("y_scale", p_sum, 0.25 * PENALTY, MUL)
+        inv_p2 = tiny("inv_p2", inv_p, 2.0, MUL)
+
+        rp = wide("rp")
+        iu2 = wide("iu2")
+        for h, l in zip(HALVES, LIST_HALVES):
+            vec.tensor_tensor(rp[:, h], r[:].indirect(slot_list[:, l]), p[:, h], MUL)
+        for h in HALVES:
+            act.activation(iu2[:, h], rp[:, h], ACT.Abs_reciprocal_sqrt)
+        rg = p
+        for h, l in zip(HALVES, LIST_HALVES):
+            act.activation(rg[:, h], r[:].indirect(slot_list[:, l]), ACT.Copy)
+
+        u = wide("u")
+        u_sum = cols("u_sum")
+        for h, s in zip(HALVES, u_sum):
+            stt(u[:, h], rp[:, h], inv_p2[:], MUL, iu2[:, h], MUL, s[:])
+        r2_sum = col("r2_sum")
+        act.activation(rp[:], r[:], ACT.Square, accum_out=r2_sum[:])
+        cu = wide("cu")
+        cu_sum = cols("cu_sum")
+        stt(cu[:, HALVES[0]], c0[:, HALVES[0]], 1.0, MUL, u[:, HALVES[0]], MUL, cu_sum[0][:])
+        z = tiny("z", u_sum[0], u_sum[1][:], ADD, res_s[:], ADD)
+        stt(cu[:, HALVES[1]], c0[:, HALVES[1]], 1.0, MUL, u[:, HALVES[1]], MUL, cu_sum[1][:])
+        inv_z = col("inv_z")
+        vec.reciprocal(inv_z[:], z[:])
+        rho = wide("rho")
+        stt(rho[:, HALVES[0]], r[:, HALVES[0]], inv_z[:], MUL, iu2[:, HALVES[0]], MUL)
+        m = tiny("m", cu_sum[0], cu_sum[1][:], ADD, inv_z[:], MUL)
+        stt(rho[:, HALVES[1]], r[:, HALVES[1]], inv_z[:], MUL, iu2[:, HALVES[1]], MUL)
+        e1 = wide("e1")
+        s1 = wide("s1")
+        for h, l in zip(HALVES, LIST_HALVES):
+            stt(e1[:, h], c0[:, h], m[:], SUB, rho[:, h], MUL)
+            act.activation(s1[:].indirect(slot_list[:, l]), e1[:, h], ACT.Copy)
+        rk = e1
+        act.activation(rk[:], r[:], ACT.Copy, scale=PENALTY)
+
+        t = wide("t")
+        stt(t[:], c0[:], m[:], SUB, u[:], MUL)
+        half_inv_z = tiny("half_inv_z", inv_z, 0.5, MUL)
+        t2 = tiny("t2", m, res_s[:], MUL, inv_z[:], MUL)
+        kappa = wide("kappa")
+        stt(kappa[:], c0[:], m[:], SUB, iu2[:], MUL)
+        z_2k = tiny("z_2k", z, 2.0 / PENALTY, MUL)
+        rt = wide("rt")
+        rt_sum = col("rt_sum")
+        stt(rt[:], t[:], half_inv_z[:], MUL, r[:], MUL, rt_sum[:])
+        r2t2 = tiny("r2t2", r2_sum, t2[:], MUL)
+        rgt = wide("rgt")
+        rgt_sum = col("rgt_sum")
+        stt(rgt[:], t[:], half_inv_z[:], MUL, rg[:], MUL, rgt_sum[:])
+        g_mean = tiny("g_mean", rt_sum, rgt_sum[:], ADD, r2t2[:], SUB)
+
+        x0 = wide("x0")
+        g = wide("g")
+        hdr = wide("hdr")
+        for h in HALVES:
+            stt(x0[:, h], s1[:, h], t2[:], SUB, r[:, h], MUL)
+        for h in HALVES:
+            stt(g[:, h], t[:, h], half_inv_z[:], MUL, x0[:, h], ADD)
+        for h in HALVES:
+            stt(hdr[:, h], g[:, h], g_mean[:], SUB, rk[:, h], MUL)
+        he1 = wide("he1")
+        for h, l in zip(HALVES, LIST_HALVES):
+            act.activation(he1[:, h], hdr[:].indirect(slot_list[:, l]), ACT.Copy)
+
+        vg = wide("vg")
+        vg_sum = col("vg_sum")
+        stt(vg[:], g[:], g_mean[:], SUB, g[:], MUL, vg_sum[:])
+        a1 = wide("a1")
+        a1_sum = col("a1_sum")
+        stt(a1[:], g[:], g_mean[:], SUB, u[:], MUL, a1_sum[:])
+        vg_k = tiny("vg_k", vg_sum, PENALTY, MUL)
+        a1_z = tiny("a1_z", a1_sum, inv_z[:], MUL, -0.5 * PENALTY, MUL)
+
+        a2 = wide("a2")
+        a2_sum = cols("a2_sum")
+        delta = wide("delta")
+        y = wide("y")
+        w_plus = wide("w_plus")
+        e5 = wide("e5")
+        s5 = wide("s5")
+        lo, hi = HALVES
+        stt(a2[:, lo], he1[:, lo], -1.0, MUL, rho[:, lo], MUL, a2_sum[0][:])
+        stt(delta[:, lo], a2[:, lo], z_2k[:], MUL, a1[:, lo], ADD)
+        stt(a2[:, hi], he1[:, hi], -1.0, MUL, rho[:, hi], MUL, a2_sum[1][:])
+        stt(y[:, lo], delta[:, lo], y_scale[:], MUL, kappa[:, lo], MUL)
+        alpha = tiny("alpha", a2_sum[0], a2_sum[1][:], ADD, a1_z[:], ADD)
+        stt(delta[:, hi], a2[:, hi], z_2k[:], MUL, a1[:, hi], ADD)
+        beta = tiny("beta", alpha, m[:], MUL, vg_k[:], ADD)
+        stt(w_plus[:, lo], c0[:, lo], alpha[:], MUL, y[:, lo], ADD)
+        stt(y[:, hi], delta[:, hi], y_scale[:], MUL, kappa[:, hi], MUL)
+        stt(e5[:, lo], w_plus[:, lo], beta[:], SUB, rho[:, lo], MUL)
+        act.activation(s5[:].indirect(slot_list[:, LIST_HALVES[0]]), e5[:, lo], ACT.Copy)
+        stt(w_plus[:, hi], c0[:, hi], alpha[:], MUL, y[:, hi], ADD)
+        w_minus = wide("w_minus")
+        stt(w_minus[:, lo], c0[:, lo], alpha[:], MUL, y[:, lo], SUB)
+        stt(e5[:, hi], w_plus[:, hi], beta[:], SUB, rho[:, hi], MUL)
+        act.activation(s5[:].indirect(slot_list[:, LIST_HALVES[1]]), e5[:, hi], ACT.Copy)
+
+        stt(w_minus[:, hi], c0[:, hi], alpha[:], MUL, y[:, hi], SUB)
+        shift = tiny("shift", beta, res_s[:], MUL, inv_z[:], MUL)
+        q1 = wide("q1")
+        stt(q1[:], vg[:], PENALTY, MUL, base_sb[:], ADD)
+        qp = wide("qp")
+        q = wide("q")
+        for h in HALVES:
+            stt(qp[:, h], w_minus[:, h], beta[:], SUB, u[:, h], MUL)
+        for h in HALVES:
+            stt(q[:, h], qp[:, h], half_inv_z[:], MUL, q1[:, h], ADD)
+
+        f = wide("f")
+        result = wide("result")
+        for h in HALVES:
+            stt(f[:, h], s5[:, h], shift[:], SUB, r[:, h], MUL)
+        for h, queue in zip(HALVES, (nc.sync, act)):
+            vec.tensor_tensor(result[:, h], f[:, h], q[:, h], ADD)
+            queue.dma_start(out[:, h], result[:, h])

@@ -21,7 +21,9 @@ SLOTS = 512
 ROWS = 128
 HALF = SLOTS // 2
 HALVES = (slice(0, HALF), slice(HALF, SLOTS))
-LIST_HALVES = (slice(0, HALF // 16), slice(HALF // 16, SLOTS // 16))
+FIRST = 160
+PIECES = (slice(0, FIRST), slice(FIRST, SLOTS))
+LATE_PIECES = (slice(SLOTS - FIRST, SLOTS), slice(0, SLOTS - FIRST))
 PENALTY = 512.0 * 2.0 * 512.0
 
 FLOPS = 2 * 2 * 512 * ROWS * SLOTS
@@ -61,35 +63,35 @@ def tile_attend_gpdirect_agreed_kernel(
         slot_list = pool.tile([P, SLOTS // 16], U16, name="slot_list")
         key_words = pool.tile([P, TOKENS], U16, name="key_words")
         val_words = pool.tile([P, TOKENS], U16, name="val_words")
-        key_bytes = pool.tile([P, TOKENS], U8, name="key_bytes", tag="key_bytes", align_bytes=64)
-        val_bytes = pool.tile([P, TOKENS], U8, name="val_bytes")
+        key_bytes = pool.tile([P, TOKENS], U8, name="key_bytes")
+        val_bytes = pool.tile([P, TOKENS], U8, name="val_bytes", tag="val_bytes")
         res = col("res")
 
-        def load_scale_rows(plane, scales, queues):
-            for quad, queue in enumerate(queues):
-                queue.dma_start(
-                    plane[32 * quad : 32 * quad + 4, :].bitcast(I32),
-                    scales[0, 4 * quad : 4 * quad + 4, :].bitcast(I32),
-                )
+        def listed(h):
+            return slot_list[:, h.start // 16 : h.stop // 16]
+
+        def load_scale_rows(plane, scales):
+            for row in range(4):
+                nc.sync.dma_start(plane[row:P:32, :].bitcast(I32), scales[0, row:16:4, :].bitcast(I32))
+
+        def load_rows(name, rows):
+            raw = pool.tile([P, PACK, ROWS], F32, name=name + "_raw", tag=name + "_raw", align_bytes=64)
+            nc.sync.dma_start(raw[:], rows.rearrange("(p j) w -> p j w", j=PACK))
+            return raw
 
         vec.memset(key_bytes[:].bitcast(I32), 0)
         vec.memset(val_bytes[:].bitcast(I32), 0)
-        def load_rows(name, rows, queue):
-            raw = pool.tile([P, PACK, ROWS], F32, name=name + "_raw", tag=name + "_staging")
-            queue.dma_start(raw[:], rows.rearrange("(p j) w -> p j w", j=PACK))
-            return raw
-
-        act.dma_start(res[:], reserve)
         nc.sync.dma_start(token_list[:], offs)
         nc.sync.dma_start(key_words[:].bitcast(I32), keys_words[0].bitcast(I32))
-        load_scale_rows(key_bytes, keys_scales, [nc.sync] * 4)
-        query_raw = load_rows("query", query, nc.sync)
-        gout_raw = load_rows("gout", gout, nc.gpsimd)
+        load_scale_rows(key_bytes, keys_scales)
+        query_raw = load_rows("query", query)
         nc.sync.dma_start(val_words[:].bitcast(I32), vals_words[0].bitcast(I32))
-        load_scale_rows(val_bytes, vals_scales, [nc.sync, nc.sync, nc.gpsimd, nc.gpsimd])
+        gout_raw = load_rows("gout", gout)
+        load_scale_rows(val_bytes, vals_scales)
         nc.sync.dma_start(slot_list[:], offs4)
-        res2 = col("res2")
-        act.activation(res2[:], res[:], ACT.Copy, scale=2.0)
+        nc.sync.dma_start(res[:], reserve)
+        base_sb = wide("base_sb")
+        nc.sync.dma_start(base_sb[:], base)
 
         def quantise(name, raw):
             grouped = pool.tile([P, ROWS, PACK], BF16, name=name + "_bf16", tag="bf16", align_bytes=64)
@@ -124,8 +126,6 @@ def tile_attend_gpdirect_agreed_kernel(
         query_mx = quantise("query", query_raw)
         a = product("a", query_mx, gather_packed("key", key_words, key_bytes, "key_got_words"))
         gout_mx = quantise("gout", gout_raw)
-        base_sb = pool.tile([P, SLOTS], F32, name="base_sb", tag="gout_staging")
-        nc.sync.dma_start(base_sb[:], base)
 
         neg_max = col("neg_max")
         vec.tensor_reduce(neg_max[:], a[:], mybir.AxisListType.X, MAX, negate=True)
@@ -133,29 +133,26 @@ def tile_attend_gpdirect_agreed_kernel(
         p_sum = col("p_sum")
         act.activation(p[:], a[:], ACT.Exp, bias=neg_max[:], accum_out=p_sum[:])
 
-        root = col("root")
-        act.activation(root[:], p_sum[:], ACT.Abs_reciprocal_sqrt)
-        res_s = col("res_s")
-        act.activation(res_s[:], res2[:], ACT.Copy, scale=root[:])
+        c0 = product("c0", gout_mx, gather_packed("val", val_words, val_bytes, "query_raw"))
 
-        c0 = product("c0", gout_mx, gather_packed("val", val_words, val_bytes, "key_bytes"))
-
-        inv_p = col("inv_p")
+        inv_p = pool.tile([P, 1], F32, name="inv_p", tag="val_bytes")
         vec.reciprocal(inv_p[:], p_sum[:])
         r = wide("r")
         vec.tensor_scalar(r[:], p[:], inv_p[:], None, MUL)
-        y_scale = tiny("y_scale", p_sum, 0.25 * PENALTY, MUL)
+        inv_p4 = tiny("inv_p4", inv_p, 4.0, MUL)
         inv_p2 = tiny("inv_p2", inv_p, 2.0, MUL)
 
+        lo, hi = HALVES
+        first, rest = PIECES
         rp = wide("rp")
         iu2 = wide("iu2")
-        for h, l in zip(HALVES, LIST_HALVES):
-            vec.tensor_tensor(rp[:, h], r[:].indirect(slot_list[:, l]), p[:, h], MUL)
         for h in HALVES:
-            act.activation(iu2[:, h], rp[:, h], ACT.Abs_reciprocal_sqrt)
+            vec.tensor_tensor(rp[:, h], r[:].indirect(listed(h)), p[:, h], MUL)
+        for h in HALVES:
+            act.activation(iu2[:, h], rp[:, h], ACT.Abs_reciprocal_sqrt, scale=inv_p4[:])
         rg = p
-        for h, l in zip(HALVES, LIST_HALVES):
-            act.activation(rg[:, h], r[:].indirect(slot_list[:, l]), ACT.Copy)
+        for h in HALVES:
+            act.activation(rg[:, h], r[:].indirect(listed(h)), ACT.Copy)
 
         u = wide("u")
         u_sum = cols("u_sum")
@@ -165,30 +162,29 @@ def tile_attend_gpdirect_agreed_kernel(
         act.activation(rp[:], r[:], ACT.Square, accum_out=r2_sum[:])
         cu = wide("cu")
         cu_sum = cols("cu_sum")
-        stt(cu[:, HALVES[0]], c0[:, HALVES[0]], 1.0, MUL, u[:, HALVES[0]], MUL, cu_sum[0][:])
-        z = tiny("z", u_sum[0], u_sum[1][:], ADD, res_s[:], ADD)
-        stt(cu[:, HALVES[1]], c0[:, HALVES[1]], 1.0, MUL, u[:, HALVES[1]], MUL, cu_sum[1][:])
+        stt(cu[:, lo], c0[:, lo], 1.0, MUL, u[:, lo], MUL, cu_sum[0][:])
+        z = tiny("z", u_sum[0], u_sum[1][:], ADD, res[:], ADD)
+        stt(cu[:, hi], c0[:, hi], 1.0, MUL, u[:, hi], MUL, cu_sum[1][:])
         inv_z = col("inv_z")
         vec.reciprocal(inv_z[:], z[:])
-        rho = wide("rho")
-        stt(rho[:, HALVES[0]], r[:, HALVES[0]], inv_z[:], MUL, iu2[:, HALVES[0]], MUL)
         m = tiny("m", cu_sum[0], cu_sum[1][:], ADD, inv_z[:], MUL)
-        stt(rho[:, HALVES[1]], r[:, HALVES[1]], inv_z[:], MUL, iu2[:, HALVES[1]], MUL)
+        rho = wide("rho")
         e1 = wide("e1")
         s1 = wide("s1")
-        for h, l in zip(HALVES, LIST_HALVES):
+        for h in PIECES:
+            stt(rho[:, h], r[:, h], inv_z[:], MUL, iu2[:, h], MUL)
+        for h in PIECES:
             stt(e1[:, h], c0[:, h], m[:], SUB, rho[:, h], MUL)
-            act.activation(s1[:].indirect(slot_list[:, l]), e1[:, h], ACT.Copy)
+            act.activation(s1[:].indirect(listed(h)), e1[:, h], ACT.Copy)
         rk = e1
         act.activation(rk[:], r[:], ACT.Copy, scale=PENALTY)
 
         t = wide("t")
         stt(t[:], c0[:], m[:], SUB, u[:], MUL)
         half_inv_z = tiny("half_inv_z", inv_z, 0.5, MUL)
-        t2 = tiny("t2", m, res_s[:], MUL, inv_z[:], MUL)
-        kappa = wide("kappa")
-        stt(kappa[:], c0[:], m[:], SUB, iu2[:], MUL)
-        z_2k = tiny("z_2k", z, 2.0 / PENALTY, MUL)
+        t2 = tiny("t2", m, res[:], MUL, inv_z[:], MUL)
+        k_inv_z = tiny("k_inv_z", inv_z, 0.5 * PENALTY, MUL)
+        neg_z2 = tiny("neg_z2", z, -2.0, MUL)
         rt = wide("rt")
         rt_sum = col("rt_sum")
         stt(rt[:], t[:], half_inv_z[:], MUL, r[:], MUL, rt_sum[:])
@@ -197,6 +193,12 @@ def tile_attend_gpdirect_agreed_kernel(
         rgt_sum = col("rgt_sum")
         stt(rgt[:], t[:], half_inv_z[:], MUL, rg[:], MUL, rgt_sum[:])
         g_mean = tiny("g_mean", rt_sum, rgt_sum[:], ADD, r2t2[:], SUB)
+        neg_cm = rg
+        act.activation(neg_cm[:], c0[:], ACT.Identity, bias=m[:], scale=-1.0)
+        centre = col("centre")
+        act.activation(centre[:], g_mean[:], ACT.Copy, scale=-0.5 * PENALTY**0.5)
+        centre_sq = col("centre_sq")
+        act.activation(centre_sq[:], centre[:], ACT.Square)
 
         x0 = wide("x0")
         g = wide("g")
@@ -207,59 +209,55 @@ def tile_attend_gpdirect_agreed_kernel(
             stt(g[:, h], t[:, h], half_inv_z[:], MUL, x0[:, h], ADD)
         for h in HALVES:
             stt(hdr[:, h], g[:, h], g_mean[:], SUB, rk[:, h], MUL)
-        he1 = wide("he1")
-        for h, l in zip(HALVES, LIST_HALVES):
-            act.activation(he1[:, h], hdr[:].indirect(slot_list[:, l]), ACT.Copy)
+        sq = wide("sq")
+        sq_sum = col("sq_sum")
+        act.activation(sq[:], g[:], ACT.Square, bias=centre[:], scale=PENALTY**0.5, accum_out=sq_sum[:])
+        he1 = pool.tile([P, HALF], F32, name="he1")
+        act.activation(he1[:], hdr[:].indirect(listed(lo)), ACT.Copy)
+        vg_k = col("vg_k")
+        act.activation(vg_k[:], centre_sq[:], ACT.Identity, bias=sq_sum[:], scale=-float(SLOTS))
 
-        vg = wide("vg")
-        vg_sum = col("vg_sum")
-        stt(vg[:], g[:], g_mean[:], SUB, g[:], MUL, vg_sum[:])
         a1 = wide("a1")
         a1_sum = col("a1_sum")
         stt(a1[:], g[:], g_mean[:], SUB, u[:], MUL, a1_sum[:])
-        vg_k = tiny("vg_k", vg_sum, PENALTY, MUL)
-        a1_z = tiny("a1_z", a1_sum, inv_z[:], MUL, -0.5 * PENALTY, MUL)
-
         a2 = wide("a2")
-        a2_sum = cols("a2_sum")
+        vec.tensor_tensor(a2[:, hi], hdr[:].indirect(listed(hi)), rho[:, hi], MUL)
+        a1_z = tiny("a1_z", a1_sum, k_inv_z[:], MUL, -2.0, MUL)
+        vec.tensor_tensor(a2[:, lo], he1[:], rho[:, lo], MUL)
         delta = wide("delta")
-        y = wide("y")
+        delta_sum = cols("delta_sum")
+        stt(delta[:, hi], a1[:, hi], k_inv_z[:], MUL, a2[:, hi], SUB, delta_sum[1][:])
+        stt(delta[:, lo], a1[:, lo], k_inv_z[:], MUL, a2[:, lo], SUB, delta_sum[0][:])
+        neg_d = wide("neg_d")
         w_plus = wide("w_plus")
+        w_minus = wide("w_minus")
         e5 = wide("e5")
         s5 = wide("s5")
-        lo, hi = HALVES
-        stt(a2[:, lo], he1[:, lo], -1.0, MUL, rho[:, lo], MUL, a2_sum[0][:])
-        stt(delta[:, lo], a2[:, lo], z_2k[:], MUL, a1[:, lo], ADD)
-        stt(a2[:, hi], he1[:, hi], -1.0, MUL, rho[:, hi], MUL, a2_sum[1][:])
-        stt(y[:, lo], delta[:, lo], y_scale[:], MUL, kappa[:, lo], MUL)
-        alpha = tiny("alpha", a2_sum[0], a2_sum[1][:], ADD, a1_z[:], ADD)
-        stt(delta[:, hi], a2[:, hi], z_2k[:], MUL, a1[:, hi], ADD)
-        beta = tiny("beta", alpha, m[:], MUL, vg_k[:], ADD)
-        stt(w_plus[:, lo], c0[:, lo], alpha[:], MUL, y[:, lo], ADD)
-        stt(y[:, hi], delta[:, hi], y_scale[:], MUL, kappa[:, hi], MUL)
-        stt(e5[:, lo], w_plus[:, lo], beta[:], SUB, rho[:, lo], MUL)
-        act.activation(s5[:].indirect(slot_list[:, LIST_HALVES[0]]), e5[:, lo], ACT.Copy)
-        stt(w_plus[:, hi], c0[:, hi], alpha[:], MUL, y[:, hi], ADD)
-        w_minus = wide("w_minus")
-        stt(w_minus[:, lo], c0[:, lo], alpha[:], MUL, y[:, lo], SUB)
-        stt(e5[:, hi], w_plus[:, hi], beta[:], SUB, rho[:, hi], MUL)
-        act.activation(s5[:].indirect(slot_list[:, LIST_HALVES[1]]), e5[:, hi], ACT.Copy)
+        stt(neg_d[:, hi], delta[:, hi], neg_z2[:], MUL, iu2[:, hi], MUL)
+        alpha = tiny("alpha", delta_sum[0], delta_sum[1][:], ADD, a1_z[:], ADD)
+        stt(neg_d[:, lo], delta[:, lo], neg_z2[:], MUL, iu2[:, lo], MUL)
+        for h in LATE_PIECES:
+            stt(w_plus[:, h], neg_d[:, h], alpha[:], SUB, neg_cm[:, h], MUL)
+        for h in LATE_PIECES:
+            stt(e5[:, h], w_plus[:, h], vg_k[:], SUB, rho[:, h], MUL)
+            act.activation(s5[:].indirect(listed(h)), e5[:, h], ACT.Copy)
 
-        stt(w_minus[:, hi], c0[:, hi], alpha[:], MUL, y[:, hi], SUB)
-        shift = tiny("shift", beta, res_s[:], MUL, inv_z[:], MUL)
-        q1 = wide("q1")
-        stt(q1[:], vg[:], PENALTY, MUL, base_sb[:], ADD)
-        qp = wide("qp")
-        q = wide("q")
+        stt(w_minus[:], neg_d[:], alpha[:], ADD, neg_cm[:], MUL)
+        beta = tiny("beta", alpha, m[:], MUL, vg_k[:], ADD)
+        q1 = w_plus
+        stt(q1[:], sq[:], centre_sq[:], SUB, base_sb[:], ADD)
+        shift = tiny("shift", beta, res[:], MUL, inv_z[:], MUL)
+        neg_qp = wide("neg_qp")
+        neg_q = wide("neg_q")
         for h in HALVES:
-            stt(qp[:, h], w_minus[:, h], beta[:], SUB, u[:, h], MUL)
+            stt(neg_qp[:, h], w_minus[:, h], vg_k[:], ADD, u[:, h], MUL)
         for h in HALVES:
-            stt(q[:, h], qp[:, h], half_inv_z[:], MUL, q1[:, h], ADD)
+            stt(neg_q[:, h], neg_qp[:, h], half_inv_z[:], MUL, q1[:, h], SUB)
 
         f = wide("f")
         result = wide("result")
         for h in HALVES:
             stt(f[:, h], s5[:, h], shift[:], SUB, r[:, h], MUL)
         for h, queue in zip(HALVES, (nc.sync, act)):
-            vec.tensor_tensor(result[:, h], f[:, h], q[:, h], ADD)
+            vec.tensor_tensor(result[:, h], f[:, h], neg_q[:, h], SUB)
             queue.dma_start(out[:, h], result[:, h])

@@ -82,8 +82,8 @@ def tile_attend_gpdirect_agreed_kernel(
         vec.memset(key_bytes[:].bitcast(I32), 0)
         vec.memset(val_bytes[:].bitcast(I32), 0)
         nc.sync.dma_start(token_list[:], offs)
-        nc.sync.dma_start(key_words[:].bitcast(I32), keys_words[0].bitcast(I32))
         load_scale_rows(key_bytes, keys_scales)
+        nc.sync.dma_start(key_words[:].bitcast(I32), keys_words[0].bitcast(I32))
         query_raw = load_rows("query", query)
         nc.sync.dma_start(val_words[:].bitcast(I32), vals_words[0].bitcast(I32))
         gout_raw = load_rows("gout", gout)
@@ -103,11 +103,12 @@ def tile_attend_gpdirect_agreed_kernel(
             )
             return codes, scales
 
-        def gather_packed(name, words, plane, words_tag):
+        def gather_packed(name, words, plane, words_tag, bytes_first):
             got_words = pool.tile([P, SLOTS], U16, name=name + "_got_words", tag=words_tag, align_bytes=64)
             got_bytes = pool.tile([P, SLOTS], U8, name=name + "_got_bytes", tag="got_bytes", align_bytes=64)
-            vec.tensor_copy(got_words[:], words[:].indirect(token_list[:]))
-            vec.tensor_copy(got_bytes[:], plane[:].indirect(token_list[:]))
+            sorts = [(got_words, words), (got_bytes, plane)]
+            for got, window in reversed(sorts) if bytes_first else sorts:
+                vec.tensor_copy(got[:], window[:].indirect(token_list[:]))
             return got_words, got_bytes
 
         def product(name, rows, columns):
@@ -124,7 +125,7 @@ def tile_attend_gpdirect_agreed_kernel(
             return acc
 
         query_mx = quantise("query", query_raw)
-        a = product("a", query_mx, gather_packed("key", key_words, key_bytes, "key_got_words"))
+        a = product("a", query_mx, gather_packed("key", key_words, key_bytes, "key_got_words", True))
         gout_mx = quantise("gout", gout_raw)
 
         neg_max = col("neg_max")
@@ -133,7 +134,7 @@ def tile_attend_gpdirect_agreed_kernel(
         p_sum = col("p_sum")
         act.activation(p[:], a[:], ACT.Exp, bias=neg_max[:], accum_out=p_sum[:])
 
-        c0 = product("c0", gout_mx, gather_packed("val", val_words, val_bytes, "query_raw"))
+        c0 = product("c0", gout_mx, gather_packed("val", val_words, val_bytes, "query_raw", False))
 
         inv_p = pool.tile([P, 1], F32, name="inv_p", tag="val_bytes")
         vec.reciprocal(inv_p[:], p_sum[:])
@@ -143,7 +144,6 @@ def tile_attend_gpdirect_agreed_kernel(
         inv_p2 = tiny("inv_p2", inv_p, 2.0, MUL)
 
         lo, hi = HALVES
-        first, rest = PIECES
         rp = wide("rp")
         iu2 = wide("iu2")
         for h in HALVES:
@@ -171,16 +171,15 @@ def tile_attend_gpdirect_agreed_kernel(
         rho = wide("rho")
         e1 = wide("e1")
         s1 = wide("s1")
+        t = wide("t")
         for h in PIECES:
             stt(rho[:, h], r[:, h], inv_z[:], MUL, iu2[:, h], MUL)
-        for h in PIECES:
+            stt(t[:, h], c0[:, h], m[:], SUB, u[:, h], MUL)
             stt(e1[:, h], c0[:, h], m[:], SUB, rho[:, h], MUL)
             act.activation(s1[:].indirect(listed(h)), e1[:, h], ACT.Copy)
         rk = e1
         act.activation(rk[:], r[:], ACT.Copy, scale=PENALTY)
 
-        t = wide("t")
-        stt(t[:], c0[:], m[:], SUB, u[:], MUL)
         half_inv_z = tiny("half_inv_z", inv_z, 0.5, MUL)
         t2 = tiny("t2", m, res[:], MUL, inv_z[:], MUL)
         k_inv_z = tiny("k_inv_z", inv_z, 0.5 * PENALTY, MUL)
@@ -195,12 +194,14 @@ def tile_attend_gpdirect_agreed_kernel(
         g_mean = tiny("g_mean", rt_sum, rgt_sum[:], ADD, r2t2[:], SUB)
         neg_cm = rg
         act.activation(neg_cm[:], c0[:], ACT.Identity, bias=m[:], scale=-1.0)
+        res_z = col("res_z")
+        act.activation(res_z[:], res[:], ACT.Copy, scale=inv_z[:])
         centre = col("centre")
         act.activation(centre[:], g_mean[:], ACT.Copy, scale=-0.5 * PENALTY**0.5)
         centre_sq = col("centre_sq")
         act.activation(centre_sq[:], centre[:], ACT.Square)
 
-        x0 = wide("x0")
+        x0 = rgt
         g = wide("g")
         hdr = wide("hdr")
         for h in HALVES:
@@ -216,6 +217,8 @@ def tile_attend_gpdirect_agreed_kernel(
         act.activation(he1[:], hdr[:].indirect(listed(lo)), ACT.Copy)
         vg_k = col("vg_k")
         act.activation(vg_k[:], centre_sq[:], ACT.Identity, bias=sq_sum[:], scale=-float(SLOTS))
+        vg_res = col("vg_res")
+        act.activation(vg_res[:], vg_k[:], ACT.Copy, scale=res_z[:])
 
         a1 = wide("a1")
         a1_sum = col("a1_sum")
@@ -235,18 +238,17 @@ def tile_attend_gpdirect_agreed_kernel(
         s5 = wide("s5")
         stt(neg_d[:, hi], delta[:, hi], neg_z2[:], MUL, iu2[:, hi], MUL)
         alpha = tiny("alpha", delta_sum[0], delta_sum[1][:], ADD, a1_z[:], ADD)
+        shift = col("shift")
+        act.activation(shift[:], alpha[:], ACT.Identity, bias=vg_res[:], scale=t2[:])
         stt(neg_d[:, lo], delta[:, lo], neg_z2[:], MUL, iu2[:, lo], MUL)
         for h in LATE_PIECES:
             stt(w_plus[:, h], neg_d[:, h], alpha[:], SUB, neg_cm[:, h], MUL)
-        for h in LATE_PIECES:
+            stt(w_minus[:, h], neg_d[:, h], alpha[:], ADD, neg_cm[:, h], MUL)
             stt(e5[:, h], w_plus[:, h], vg_k[:], SUB, rho[:, h], MUL)
             act.activation(s5[:].indirect(listed(h)), e5[:, h], ACT.Copy)
 
-        stt(w_minus[:], neg_d[:], alpha[:], ADD, neg_cm[:], MUL)
-        beta = tiny("beta", alpha, m[:], MUL, vg_k[:], ADD)
         q1 = w_plus
         stt(q1[:], sq[:], centre_sq[:], SUB, base_sb[:], ADD)
-        shift = tiny("shift", beta, res[:], MUL, inv_z[:], MUL)
         neg_qp = wide("neg_qp")
         neg_q = wide("neg_q")
         for h in HALVES:
@@ -254,7 +256,7 @@ def tile_attend_gpdirect_agreed_kernel(
         for h in HALVES:
             stt(neg_q[:, h], neg_qp[:, h], half_inv_z[:], MUL, q1[:, h], SUB)
 
-        f = wide("f")
+        f = neg_qp
         result = wide("result")
         for h in HALVES:
             stt(f[:, h], s5[:, h], shift[:], SUB, r[:, h], MUL)

from contextlib import ExitStack

import concourse.mybir as mybir

F32 = mybir.dt.float32
BF16 = mybir.dt.bfloat16
I32 = mybir.dt.int32
U32 = mybir.dt.uint32
U16 = mybir.dt.uint16
U8 = mybir.dt.uint8
FP8X4 = mybir.dt.float8_e4m3fn_x4
FP4X4 = mybir.dt.float4_e2m1fn_x4
ALU = mybir.AluOpType
ACT = mybir.ActivationFunctionType
ADD, SUB, MUL, MAX = ALU.add, ALU.subtract, ALU.mult, ALU.max

P = 128
PACK = 4
TOKENS = 2048
SLOTS = 512
ROWS = 128
HALF = SLOTS // 2
HALVES = (slice(0, HALF), slice(HALF, SLOTS))
FIRST = 160
PIECES = (slice(0, FIRST), slice(FIRST, SLOTS))
LATE_PIECES = (slice(SLOTS - FIRST, SLOTS), slice(0, SLOTS - FIRST))
PENALTY = 512.0 * 2.0 * 512.0

FLOPS = 2 * 2 * 512 * ROWS * SLOTS


def tile_attend_gpdirect_agreed_kernel(
    tc, query, keys_words, keys_scales, reserve, gout, vals_words, vals_scales, base, offs4, offs, out
):
    nc = tc.nc
    vec, act = nc.vector, nc.scalar

    with ExitStack() as ctx:
        pool = ctx.enter_context(tc.tile_pool(name="sbuf", bufs=1))
        psum = ctx.enter_context(tc.psum_pool(name="psum", bufs=1))

        def wide(name):
            return pool.tile([P, SLOTS], F32, name=name)

        def col(name):
            return pool.tile([P, 1], F32, name=name)

        def cols(name):
            return [col(name + "_lo"), col(name + "_hi")]

        def stt(dst, in0, scalar, op0, in1, op1, accum=None):
            vec.scalar_tensor_tensor(dst, in0, scalar, in1, op0, op1, accum_out=accum)

        def tiny(name, in0, s1, op0, s2=None, op1=None):
            dst = col(name)
            if op1 is None:
                vec.tensor_scalar(dst[:], in0[:], s1, None, op0)
            else:
                vec.tensor_scalar(dst[:], in0[:], s1, s2, op0, op1)
            return dst

        token_list = pool.tile([P, SLOTS // 16], U16, name="token_list")
        slot_list = pool.tile([P, SLOTS // 16], U16, name="slot_list")
        key_words = pool.tile([P, TOKENS], U16, name="key_words")
        val_words = pool.tile([P, TOKENS], U16, name="val_words")
        key_bytes = pool.tile([P, TOKENS], U8, name="key_bytes")
        val_bytes = pool.tile([P, TOKENS], U8, name="val_bytes", tag="val_bytes")
        res = col("res")

        def listed(h):
            return slot_list[:, h.start // 16 : h.stop // 16]

        def load_scale_rows(plane, scales):
            for row in range(4):
                nc.sync.dma_start(plane[row:P:32, :].bitcast(I32), scales[0, row:16:4, :].bitcast(I32))

        def load_rows(name, rows):
            raw = pool.tile([P, PACK, ROWS], F32, name=name + "_raw", tag=name + "_raw", align_bytes=64)
            nc.sync.dma_start(raw[:], rows.rearrange("(p j) w -> p j w", j=PACK))
            return raw

        vec.memset(key_bytes[:].bitcast(I32), 0)
        vec.memset(val_bytes[:].bitcast(I32), 0)
        nc.sync.dma_start(token_list[:], offs)
        load_scale_rows(key_bytes, keys_scales)
        nc.sync.dma_start(key_words[:].bitcast(I32), keys_words[0].bitcast(I32))
        query_raw = load_rows("query", query)
        nc.sync.dma_start(val_words[:].bitcast(I32), vals_words[0].bitcast(I32))
        gout_raw = load_rows("gout", gout)
        load_scale_rows(val_bytes, vals_scales)
        nc.sync.dma_start(slot_list[:], offs4)
        nc.sync.dma_start(res[:], reserve)
        base_sb = wide("base_sb")
        nc.sync.dma_start(base_sb[:], base)

        def quantise(name, raw):
            grouped = pool.tile([P, ROWS, PACK], BF16, name=name + "_bf16", tag="bf16", align_bytes=64)
            codes = pool.tile([P, ROWS], U32, name=name + "_codes", align_bytes=64)
            scales = pool.tile([P, ROWS], U8, name=name + "_scales", align_bytes=64)
            act.activation(grouped[:], raw[:].rearrange("p j w -> p w j"), ACT.Copy)
            vec.quantize_mx(
                out=codes[:].bitcast(FP8X4), scales=scales[:], in_=grouped[:].rearrange("p w j -> p (w j)")
            )
            return codes, scales

        def gather_packed(name, words, plane, words_tag, bytes_first):
            got_words = pool.tile([P, SLOTS], U16, name=name + "_got_words", tag=words_tag, align_bytes=64)
            got_bytes = pool.tile([P, SLOTS], U8, name=name + "_got_bytes", tag="got_bytes", align_bytes=64)
            sorts = [(got_words, words), (got_bytes, plane)]
            for got, window in reversed(sorts) if bytes_first else sorts:
                vec.tensor_copy(got[:], window[:].indirect(token_list[:]))
            return got_words, got_bytes

        def product(name, rows, columns):
            acc = psum.tile([P, SLOTS], F32, name=name)
            nc.tensor.matmul_mx(
                out=acc[:],
                lhsT=rows[0][:].bitcast(FP8X4),
                lhsT_scale=rows[1][:],
                rhs=columns[0][:].bitcast(FP4X4),
                rhs_scale=columns[1][:],
                start=True,
                stop=True,
            )
            return acc

        query_mx = quantise("query", query_raw)
        a = product("a", query_mx, gather_packed("key", key_words, key_bytes, "key_got_words", True))
        gout_mx = quantise("gout", gout_raw)

        neg_max = col("neg_max")
        vec.tensor_reduce(neg_max[:], a[:], mybir.AxisListType.X, MAX, negate=True)
        p = wide("p")
        p_sum = col("p_sum")
        act.activation(p[:], a[:], ACT.Exp, bias=neg_max[:], accum_out=p_sum[:])

        c0 = product("c0", gout_mx, gather_packed("val", val_words, val_bytes, "query_raw", False))

        inv_p = pool.tile([P, 1], F32, name="inv_p", tag="val_bytes")
        vec.reciprocal(inv_p[:], p_sum[:])
        r = wide("r")
        vec.tensor_scalar(r[:], p[:], inv_p[:], None, MUL)
        inv_p4 = tiny("inv_p4", inv_p, 4.0, MUL)
        inv_p2 = tiny("inv_p2", inv_p, 2.0, MUL)

        lo, hi = HALVES
        rp = wide("rp")
        iu2 = wide("iu2")
        for h in HALVES:
            vec.tensor_tensor(rp[:, h], r[:].indirect(listed(h)), p[:, h], MUL)
        for h in HALVES:
            act.activation(iu2[:, h], rp[:, h], ACT.Abs_reciprocal_sqrt, scale=inv_p4[:])
        rg = p
        for h in HALVES:
            act.activation(rg[:, h], r[:].indirect(listed(h)), ACT.Copy)

        u = wide("u")
        u_sum = cols("u_sum")
        for h, s in zip(HALVES, u_sum):
            stt(u[:, h], rp[:, h], inv_p2[:], MUL, iu2[:, h], MUL, s[:])
        r2_sum = col("r2_sum")
        act.activation(rp[:], r[:], ACT.Square, accum_out=r2_sum[:])
        cu = wide("cu")
        cu_sum = cols("cu_sum")
        stt(cu[:, lo], c0[:, lo], 1.0, MUL, u[:, lo], MUL, cu_sum[0][:])
        z = tiny("z", u_sum[0], u_sum[1][:], ADD, res[:], ADD)
        stt(cu[:, hi], c0[:, hi], 1.0, MUL, u[:, hi], MUL, cu_sum[1][:])
        inv_z = col("inv_z")
        vec.reciprocal(inv_z[:], z[:])
        m = tiny("m", cu_sum[0], cu_sum[1][:], ADD, inv_z[:], MUL)
        rho = wide("rho")
        e1 = wide("e1")
        s1 = wide("s1")
        t = wide("t")
        for h in PIECES:
            stt(rho[:, h], r[:, h], inv_z[:], MUL, iu2[:, h], MUL)
            stt(t[:, h], c0[:, h], m[:], SUB, u[:, h], MUL)
            stt(e1[:, h], c0[:, h], m[:], SUB, rho[:, h], MUL)
            act.activation(s1[:].indirect(listed(h)), e1[:, h], ACT.Copy)
        rk = e1
        act.activation(rk[:], r[:], ACT.Copy, scale=PENALTY)

        half_inv_z = tiny("half_inv_z", inv_z, 0.5, MUL)
        t2 = tiny("t2", m, res[:], MUL, inv_z[:], MUL)
        k_inv_z = tiny("k_inv_z", inv_z, 0.5 * PENALTY, MUL)
        neg_z2 = tiny("neg_z2", z, -2.0, MUL)
        rt = wide("rt")
        rt_sum = col("rt_sum")
        stt(rt[:], t[:], half_inv_z[:], MUL, r[:], MUL, rt_sum[:])
        r2t2 = tiny("r2t2", r2_sum, t2[:], MUL)
        rgt = wide("rgt")
        rgt_sum = col("rgt_sum")
        stt(rgt[:], t[:], half_inv_z[:], MUL, rg[:], MUL, rgt_sum[:])
        g_mean = tiny("g_mean", rt_sum, rgt_sum[:], ADD, r2t2[:], SUB)
        neg_cm = rg
        act.activation(neg_cm[:], c0[:], ACT.Identity, bias=m[:], scale=-1.0)
        res_z = col("res_z")
        act.activation(res_z[:], res[:], ACT.Copy, scale=inv_z[:])
        centre = col("centre")
        act.activation(centre[:], g_mean[:], ACT.Copy, scale=-0.5 * PENALTY**0.5)
        centre_sq = col("centre_sq")
        act.activation(centre_sq[:], centre[:], ACT.Square)

        x0 = rgt
        g = wide("g")
        hdr = wide("hdr")
        for h in HALVES:
            stt(x0[:, h], s1[:, h], t2[:], SUB, r[:, h], MUL)
        for h in HALVES:
            stt(g[:, h], t[:, h], half_inv_z[:], MUL, x0[:, h], ADD)
        for h in HALVES:
            stt(hdr[:, h], g[:, h], g_mean[:], SUB, rk[:, h], MUL)
        sq = wide("sq")
        sq_sum = col("sq_sum")
        act.activation(sq[:], g[:], ACT.Square, bias=centre[:], scale=PENALTY**0.5, accum_out=sq_sum[:])
        he1 = pool.tile([P, HALF], F32, name="he1")
        act.activation(he1[:], hdr[:].indirect(listed(lo)), ACT.Copy)
        vg_k = col("vg_k")
        act.activation(vg_k[:], centre_sq[:], ACT.Identity, bias=sq_sum[:], scale=-float(SLOTS))
        vg_res = col("vg_res")
        act.activation(vg_res[:], vg_k[:], ACT.Copy, scale=res_z[:])

        a1 = wide("a1")
        a1_sum = col("a1_sum")
        stt(a1[:], g[:], g_mean[:], SUB, u[:], MUL, a1_sum[:])
        a2 = wide("a2")
        vec.tensor_tensor(a2[:, hi], hdr[:].indirect(listed(hi)), rho[:, hi], MUL)
        a1_z = tiny("a1_z", a1_sum, k_inv_z[:], MUL, -2.0, MUL)
        vec.tensor_tensor(a2[:, lo], he1[:], rho[:, lo], MUL)
        delta = wide("delta")
        delta_sum = cols("delta_sum")
        stt(delta[:, hi], a1[:, hi], k_inv_z[:], MUL, a2[:, hi], SUB, delta_sum[1][:])
        stt(delta[:, lo], a1[:, lo], k_inv_z[:], MUL, a2[:, lo], SUB, delta_sum[0][:])
        neg_d = wide("neg_d")
        w_plus = wide("w_plus")
        w_minus = wide("w_minus")
        e5 = wide("e5")
        s5 = wide("s5")
        stt(neg_d[:, hi], delta[:, hi], neg_z2[:], MUL, iu2[:, hi], MUL)
        alpha = tiny("alpha", delta_sum[0], delta_sum[1][:], ADD, a1_z[:], ADD)
        shift = col("shift")
        act.activation(shift[:], alpha[:], ACT.Identity, bias=vg_res[:], scale=t2[:])
        stt(neg_d[:, lo], delta[:, lo], neg_z2[:], MUL, iu2[:, lo], MUL)
        for h in LATE_PIECES:
            stt(w_plus[:, h], neg_d[:, h], alpha[:], SUB, neg_cm[:, h], MUL)
            stt(w_minus[:, h], neg_d[:, h], alpha[:], ADD, neg_cm[:, h], MUL)
            stt(e5[:, h], w_plus[:, h], vg_k[:], SUB, rho[:, h], MUL)
            act.activation(s5[:].indirect(listed(h)), e5[:, h], ACT.Copy)

        q1 = w_plus
        stt(q1[:], sq[:], centre_sq[:], SUB, base_sb[:], ADD)
        neg_qp = wide("neg_qp")
        neg_q = wide("neg_q")
        for h in HALVES:
            stt(neg_qp[:, h], w_minus[:, h], vg_k[:], ADD, u[:, h], MUL)
        for h in HALVES:
            stt(neg_q[:, h], neg_qp[:, h], half_inv_z[:], MUL, q1[:, h], SUB)

        f = neg_qp
        result = wide("result")
        for h in HALVES:
            stt(f[:, h], s5[:, h], shift[:], SUB, r[:, h], MUL)
        for h, queue in zip(HALVES, (nc.sync, act)):
            vec.tensor_tensor(result[:, h], f[:, h], neg_q[:, h], SUB)
            queue.dma_start(out[:, h], result[:, h])
